import numpy as np
import ml_dtypes

BF16 = ml_dtypes.bfloat16


def bf(x):
    return np.asarray(x, np.float32).astype(BF16)


def f32(x):
    return np.asarray(x, np.float32)


def f64(x):
    return np.asarray(x).astype(np.float64)


def striped(idx):
    return np.tile(idx.reshape(-1, 16).T, (8, 1))


S, K, M, N = 512, 128, 128, 384


def setup_inputs():
    return {"base": bf(np.random.standard_normal((M, S))), "x": bf(np.random.standard_normal((K, N))), "w": bf(np.random.standard_normal((K, M)) / np.sqrt(K)), "b": f32(0.5 * np.random.standard_normal((M, 1))), "offs": striped(np.random.permutation(S)[:N])}


def reference(base, x, w, b, offs):
    idx = offs[:16].T.reshape(-1)
    z = f64(base).copy()
    z[:, idx] = f64(w).T @ f64(x)
    return np.maximum(z + f64(b), 0.0)

@@ -1,0 +1,42 @@
+import concourse.mybir as mybir
+from concourse.masks import make_identity
+
+P = 128
+TOKENS = 512
+PICKED = 384
+FLOPS = 2 * P * P * PICKED
+
+BF16, F32, U16 = mybir.dt.bfloat16, mybir.dt.float32, mybir.dt.uint16
+ADD, MAX = mybir.AluOpType.add, mybir.AluOpType.max
+
+
+def tile_scatter_matmul_kernel(tc, base, x, w, b, offs, out):
+    nc = tc.nc
+    with (
+        tc.tile_pool(name="held", bufs=1) as held,
+        tc.psum_pool(name="psum", bufs=1) as psum,
+    ):
+        offsets = held.tile([P, PICKED // 16], U16, name="offsets")
+        nc.sync.dma_start(offsets[:], offs)
+        base_sb = held.tile([P, TOKENS], BF16, name="base_sb")
+        nc.scalar.dma_start(base_sb[:], base)
+        x_sb = held.tile([P, PICKED], BF16, name="x_sb")
+        nc.sync.dma_start(x_sb[:], x)
+        w_sb = held.tile([P, P], BF16, name="w_sb")
+        nc.scalar.dma_start(w_sb[:], w)
+
+        ident = held.tile([P, P], BF16, name="ident")
+        make_identity(nc, ident[:])
+        bias = held.tile([P, 1], F32, name="bias")
+        nc.gpsimd.dma_start(bias[:], b)
+
+        window = psum.tile([P, TOKENS], F32, name="window")
+        nc.tensor.matmul(window[:], ident[:], base_sb[:], start=True, stop=True)
+
+        nc.tensor.matmul(
+            window[:].indirect(offsets[:]), w_sb[:], x_sb[:], start=True, stop=True
+        )
+
+        result = held.tile([P, TOKENS], F32, name="result")
+        nc.vector.tensor_scalar(result[:], window[:], bias[:, 0:1], 0.0, ADD, MAX)
+        nc.sync.dma_start(out, result[:])

@@ -24,11 +24,11 @@ def tile_scatter_matmul_kernel(tc, base, x, w, b, offs, out):
         nc.sync.dma_start(x_sb[:], x)
         w_sb = held.tile([P, P], BF16, name="w_sb")
         nc.scalar.dma_start(w_sb[:], w)
+        bias = held.tile([P, 1], F32, name="bias")
+        nc.sync.dma_start(bias[:], b)
 
         ident = held.tile([P, P], BF16, name="ident")
         make_identity(nc, ident[:])
-        bias = held.tile([P, 1], F32, name="bias")
-        nc.gpsimd.dma_start(bias[:], b)
 
         window = psum.tile([P, TOKENS], F32, name="window")
         nc.tensor.matmul(window[:], ident[:], base_sb[:], start=True, stop=True)

@@ -18,14 +18,14 @@ def tile_scatter_matmul_kernel(tc, base, x, w, b, offs, out):
     ):
         offsets = held.tile([P, PICKED // 16], U16, name="offsets")
         nc.sync.dma_start(offsets[:], offs)
-        base_sb = held.tile([P, TOKENS], BF16, name="base_sb")
-        nc.scalar.dma_start(base_sb[:], base)
-        x_sb = held.tile([P, PICKED], BF16, name="x_sb")
-        nc.sync.dma_start(x_sb[:], x)
-        w_sb = held.tile([P, P], BF16, name="w_sb")
-        nc.scalar.dma_start(w_sb[:], w)
         bias = held.tile([P, 1], F32, name="bias")
         nc.sync.dma_start(bias[:], b)
+        base_sb = held.tile([P, TOKENS], BF16, name="base_sb")
+        nc.scalar.dma_start(base_sb[:], base)
+        w_sb = held.tile([P, P], BF16, name="w_sb")
+        nc.scalar.dma_start(w_sb[:], w)
+        x_sb = held.tile([P, PICKED], BF16, name="x_sb")
+        nc.scalar.dma_start(x_sb[:], x)
 
         ident = held.tile([P, P], BF16, name="ident")
         make_identity(nc, ident[:])

@@ -3,6 +3,7 @@ from concourse.masks import make_identity
 
 P = 128
 TOKENS = 512
+HALF = TOKENS // 2
 PICKED = 384
 FLOPS = 2 * P * P * PICKED
 
@@ -18,14 +19,14 @@ def tile_scatter_matmul_kernel(tc, base, x, w, b, offs, out):
     ):
         offsets = held.tile([P, PICKED // 16], U16, name="offsets")
         nc.sync.dma_start(offsets[:], offs)
-        bias = held.tile([P, 1], F32, name="bias")
-        nc.sync.dma_start(bias[:], b)
         base_sb = held.tile([P, TOKENS], BF16, name="base_sb")
         nc.scalar.dma_start(base_sb[:], base)
+        x_sb = held.tile([P, PICKED], BF16, name="x_sb")
+        nc.sync.dma_start(x_sb[:], x)
         w_sb = held.tile([P, P], BF16, name="w_sb")
         nc.scalar.dma_start(w_sb[:], w)
-        x_sb = held.tile([P, PICKED], BF16, name="x_sb")
-        nc.scalar.dma_start(x_sb[:], x)
+        bias = held.tile([P, 1], F32, name="bias")
+        nc.sync.dma_start(bias[:], b)
 
         ident = held.tile([P, P], BF16, name="ident")
         make_identity(nc, ident[:])
@@ -38,5 +39,9 @@ def tile_scatter_matmul_kernel(tc, base, x, w, b, offs, out):
         )
 
         result = held.tile([P, TOKENS], F32, name="result")
-        nc.vector.tensor_scalar(result[:], window[:], bias[:, 0:1], 0.0, ADD, MAX)
-        nc.sync.dma_start(out, result[:])
+        for half, queue in enumerate((nc.sync, nc.scalar)):
+            cols = slice(half * HALF, (half + 1) * HALF)
+            nc.vector.tensor_scalar(
+                result[:, cols], window[:, cols], bias[:, 0:1], 0.0, ADD, MAX
+            )
+            queue.dma_start(out[:, cols], result[:, cols])

@@ -3,7 +3,6 @@ from concourse.masks import make_identity
 
 P = 128
 TOKENS = 512
-HALF = TOKENS // 2
 PICKED = 384
 FLOPS = 2 * P * P * PICKED
 
@@ -17,14 +16,14 @@ def tile_scatter_matmul_kernel(tc, base, x, w, b, offs, out):
         tc.tile_pool(name="held", bufs=1) as held,
         tc.psum_pool(name="psum", bufs=1) as psum,
     ):
-        offsets = held.tile([P, PICKED // 16], U16, name="offsets")
-        nc.sync.dma_start(offsets[:], offs)
         base_sb = held.tile([P, TOKENS], BF16, name="base_sb")
-        nc.scalar.dma_start(base_sb[:], base)
+        nc.sync.dma_start(base_sb[:], base)
         x_sb = held.tile([P, PICKED], BF16, name="x_sb")
         nc.sync.dma_start(x_sb[:], x)
         w_sb = held.tile([P, P], BF16, name="w_sb")
-        nc.scalar.dma_start(w_sb[:], w)
+        nc.sync.dma_start(w_sb[:], w)
+        offsets = held.tile([P, PICKED // 16], U16, name="offsets")
+        nc.sync.dma_start(offsets[:], offs)
         bias = held.tile([P, 1], F32, name="bias")
         nc.sync.dma_start(bias[:], b)
 
@@ -39,9 +38,5 @@ def tile_scatter_matmul_kernel(tc, base, x, w, b, offs, out):
         )
 
         result = held.tile([P, TOKENS], F32, name="result")
-        for half, queue in enumerate((nc.sync, nc.scalar)):
-            cols = slice(half * HALF, (half + 1) * HALF)
-            nc.vector.tensor_scalar(
-                result[:, cols], window[:, cols], bias[:, 0:1], 0.0, ADD, MAX
-            )
-            queue.dma_start(out[:, cols], result[:, cols])
+        nc.vector.tensor_scalar(result[:], window[:], bias[:, 0:1], 0.0, ADD, MAX)
+        nc.sync.dma_start(out, result[:])

@@ -5,6 +5,7 @@ P = 128
 TOKENS = 512
 PICKED = 384
 FLOPS = 2 * P * P * PICKED
+WARMUPS = 4
 
 BF16, F32, U16 = mybir.dt.bfloat16, mybir.dt.float32, mybir.dt.uint16
 ADD, MAX = mybir.AluOpType.add, mybir.AluOpType.max
@@ -26,6 +27,12 @@ def tile_scatter_matmul_kernel(tc, base, x, w, b, offs, out):
         nc.sync.dma_start(offsets[:], offs)
         bias = held.tile([P, 1], F32, name="bias")
         nc.sync.dma_start(bias[:], b)
+
+        zeros = held.tile([P, TOKENS], BF16, name="zeros")
+        nc.vector.memset(zeros[:], 0.0)
+        spare = psum.tile([P, TOKENS], F32, name="spare")
+        for _ in range(WARMUPS):
+            nc.tensor.matmul(spare[:], zeros[:, 0:P], zeros[:], start=True, stop=True)
 
         ident = held.tile([P, P], BF16, name="ident")
         make_identity(nc, ident[:])

@@ -5,7 +5,7 @@ P = 128
 TOKENS = 512
 PICKED = 384
 FLOPS = 2 * P * P * PICKED
-WARMUPS = 4
+WARMUPS = 10
 
 BF16, F32, U16 = mybir.dt.bfloat16, mybir.dt.float32, mybir.dt.uint16
 ADD, MAX = mybir.AluOpType.add, mybir.AluOpType.max
@@ -28,11 +28,11 @@ def tile_scatter_matmul_kernel(tc, base, x, w, b, offs, out):
         bias = held.tile([P, 1], F32, name="bias")
         nc.sync.dma_start(bias[:], b)
 
-        zeros = held.tile([P, TOKENS], BF16, name="zeros")
+        zeros = held.tile([P, P], BF16, name="zeros")
         nc.vector.memset(zeros[:], 0.0)
-        spare = psum.tile([P, TOKENS], F32, name="spare")
+        spare = psum.tile([P, P], F32, name="spare")
         for _ in range(WARMUPS):
-            nc.tensor.matmul(spare[:], zeros[:, 0:P], zeros[:], start=True, stop=True)
+            nc.tensor.matmul(spare[:], zeros[:], zeros[:], start=True, stop=True)
 
         ident = held.tile([P, P], BF16, name="ident")
         make_identity(nc, ident[:])

@@ -35,7 +35,8 @@ def tile_scatter_matmul_kernel(tc, base, x, w, b, offs, out):
             nc.tensor.matmul(spare[:], zeros[:], zeros[:], start=True, stop=True)
 
         ident = held.tile([P, P], BF16, name="ident")
-        make_identity(nc, ident[:])
+        nc.vector.memset(ident[:], 0.0)
+        make_identity(nc, ident[:], nomemset=True)
 
         window = psum.tile([P, TOKENS], F32, name="window")
         nc.tensor.matmul(window[:], ident[:], base_sb[:], start=True, stop=True)

import concourse.mybir as mybir
from concourse.masks import make_identity

P = 128
TOKENS = 512
PICKED = 384
FLOPS = 2 * P * P * PICKED
WARMUPS = 10

BF16, F32, U16 = mybir.dt.bfloat16, mybir.dt.float32, mybir.dt.uint16
ADD, MAX = mybir.AluOpType.add, mybir.AluOpType.max


def tile_scatter_matmul_kernel(tc, base, x, w, b, offs, out):
    nc = tc.nc
    with (
        tc.tile_pool(name="held", bufs=1) as held,
        tc.psum_pool(name="psum", bufs=1) as psum,
    ):
        base_sb = held.tile([P, TOKENS], BF16, name="base_sb")
        nc.sync.dma_start(base_sb[:], base)
        x_sb = held.tile([P, PICKED], BF16, name="x_sb")
        nc.sync.dma_start(x_sb[:], x)
        w_sb = held.tile([P, P], BF16, name="w_sb")
        nc.sync.dma_start(w_sb[:], w)
        offsets = held.tile([P, PICKED // 16], U16, name="offsets")
        nc.sync.dma_start(offsets[:], offs)
        bias = held.tile([P, 1], F32, name="bias")
        nc.sync.dma_start(bias[:], b)

        zeros = held.tile([P, P], BF16, name="zeros")
        nc.vector.memset(zeros[:], 0.0)
        spare = psum.tile([P, P], F32, name="spare")
        for _ in range(WARMUPS):
            nc.tensor.matmul(spare[:], zeros[:], zeros[:], start=True, stop=True)

        ident = held.tile([P, P], BF16, name="ident")
        nc.vector.memset(ident[:], 0.0)
        make_identity(nc, ident[:], nomemset=True)

        window = psum.tile([P, TOKENS], F32, name="window")
        nc.tensor.matmul(window[:], ident[:], base_sb[:], start=True, stop=True)

        nc.tensor.matmul(
            window[:].indirect(offsets[:]), w_sb[:], x_sb[:], start=True, stop=True
        )

        result = held.tile([P, TOKENS], F32, name="result")
        nc.vector.tensor_scalar(result[:], window[:], bias[:, 0:1], 0.0, ADD, MAX)
        nc.sync.dma_start(out, result[:])
